import numpy as np
import ml_dtypes


def mxq(x, axis, fmt="e4m3"):
    dtype, down = {"e4m3": (ml_dtypes.float8_e4m3fn, 7), "e5m2": (ml_dtypes.float8_e5m2, 14)}[fmt]
    v = np.moveaxis(np.asarray(x, np.float32).astype(ml_dtypes.bfloat16).astype(np.float64), axis, -1)
    blocks = v.reshape(v.shape[:-1] + (-1, 32))
    amax = np.abs(blocks).max(-1, keepdims=True)
    byte = np.maximum(np.where(amax > 0, np.frexp(amax)[1] - 1 + 127, 0) - down, 1)
    scale = np.exp2(byte - 127.0)
    codes = (blocks / scale).astype(np.float32).astype(dtype).astype(np.float64)
    return np.moveaxis((codes * scale).reshape(v.shape), -1, axis)


WIDE = False


def mx_kscale(k):
    if not WIDE:
        return np.ones(k)
    levels = np.array([10, -10, 5, -5, 0])
    if k % 512:
        return np.exp2(np.random.permutation(np.resize(levels, k // 32))).repeat(32)
    a = np.empty((k // 512, 16))
    for p in range(k // 512):
        a[p, :8] = np.random.permutation(np.resize(levels, 8))
        for g in range(8):
            far = levels[np.abs(levels - a[p, g]) >= 10]
            a[p, g + 8] = far[np.random.randint(len(far))]
    return np.exp2(a.ravel()).repeat(32)


def f64(x):
    return np.asarray(x).astype(np.float64)


def striped(idx):
    return np.tile(idx.reshape(-1, 16).T, (8, 1)).astype(np.uint16)


def unstriped(offs):
    return offs[:16].T.reshape(-1).astype(np.int64)


def striped8(idx):
    return np.concatenate([x.reshape(-1, 16).T for x in idx]).astype(np.uint16)


def runs(offs, k):
    lists = np.stack([offs[16 * r : 16 * r + 16].T.reshape(-1) for r in range(8)]).astype(np.int64)
    return lists[np.arange(k) % 512 // 64]


def pack_weight(w):
    k, n = w.shape
    w = f64(np.asarray(w, np.float32).astype(ml_dtypes.bfloat16)).reshape(k // 32, 32, n)
    amax = np.abs(w).max(1)
    byte = np.clip(np.where(amax > 0, np.frexp(amax)[1] - 1 + 127 - 7, 1), 1, 254)
    scaled = (w * np.exp2(127.0 - byte)[:, None, :]).reshape(k, n).astype(np.float32)
    words = np.ascontiguousarray(scaled.reshape(k // 512, 128, 4, n).transpose(0, 1, 3, 2)).astype(ml_dtypes.float8_e4m3fn).view(np.uint8)
    return words, np.ascontiguousarray(byte.astype(np.uint8).reshape(k // 512, 16, n))


def unpack_weight(words, scales):
    g, p, n, _ = words.shape
    vals = np.ascontiguousarray(words).view(ml_dtypes.float8_e4m3fn).astype(np.float64) * np.repeat(np.exp2(scales.astype(np.float64) - 127.0), 8, axis=1)[..., None]
    return vals.transpose(0, 1, 3, 2).reshape(g * 512, n)


def sigmoid(v):
    return 1.0 / (1.0 + np.exp(-np.maximum(v, -700.0)))

def planes(y):
    n, m = y.shape
    v = y.astype(np.float32).astype(ml_dtypes.bfloat16).astype(np.float64).reshape(n // 32, 32, m)
    top = np.abs(v).max(1)
    byte = np.clip(np.where(top > 0, np.frexp(top)[1] - 1 + 127 - 7, 1), 1, 254)
    codes = (v * np.exp2(127.0 - byte)[:, None, :]).reshape(n, m).astype(np.float32).astype(ml_dtypes.float8_e4m3fn).view(np.uint8)
    words = codes.reshape(n // 512, 128, 4, m).transpose(0, 1, 3, 2)
    return np.ascontiguousarray(words), np.ascontiguousarray(byte.astype(np.uint8).reshape(n // 512, 16, m))


K, T, S, N, H, U = 512, 2048, 512, 512, 512, 1024


def setup_inputs():
    n = np.random.standard_normal
    s = mx_kscale(K)[:, None]
    u = mx_kscale(H)
    packed_xT = pack_weight(n((K, T)) * s)
    packed_w1 = pack_weight(n((K, H)) / np.sqrt(K) / s)
    packed_w2 = pack_weight(n((H, N)) / np.sqrt(H) / u[:, None])
    return {
        "x_words": packed_xT[0],
        "x_scales": packed_xT[1],
        "w1_words": packed_w1[0],
        "w1_scales": packed_w1[1],
        "gn": (np.random.uniform(0.5, 1.5, (H, 1)) * u[:, None]).astype(np.float32),
        "w2_words": packed_w2[0],
        "w2_scales": packed_w2[1],
        "mem": n((N, U)).astype(np.float32),
        "offs": striped(np.random.permutation(T)[:S]),
        "n1": striped8(np.stack([np.random.permutation(S) for _ in range(8)])),
        "n2": striped8(np.stack([np.random.permutation(S) for _ in range(8)])),
        "n3": striped8(np.stack([np.random.permutation(S) for _ in range(8)])),
        "n4": striped8(np.stack([np.random.permutation(U)[:S] for _ in range(8)])),
        "n5": striped8(np.stack([np.random.permutation(U) for _ in range(8)])),
    }


def reference(x_words, x_scales, w1_words, w1_scales, gn, w2_words, w2_scales, mem, offs, n1, n2, n3, n4, n5):
    xq = unpack_weight(x_words, x_scales)[:, unstriped(offs)]
    y = unpack_weight(w1_words, w1_scales).T @ xq
    pa = y[np.arange(H)[:, None], runs(n1, H)]
    z = f64(gn) * (pa + (sigmoid(y[np.arange(H)[:, None], runs(n2, H)])) * (y[np.arange(H)[:, None], runs(n3, H)] - pa))
    h = unpack_weight(w2_words, w2_scales).T @ mxq(z, 0, "e4m3")
    pg = f64(mem).copy()
    pg[np.arange(N)[:, None], runs(n4, N)] = h
    out_0 = pg - (0.5 * (pg[np.arange(N)[:, None], runs(n5, N)]))
    return (out_0,) + planes(out_0)

@@ -1,0 +1,214 @@
+from contextlib import ExitStack
+
+import concourse.mybir as mybir
+
+K, T, S, N, H, U = 512, 2048, 512, 512, 512, 1024
+FLOPS = 2 * K * H * S + 2 * H * N * S
+
+F32 = mybir.dt.float32
+BF16 = mybir.dt.bfloat16
+I32 = mybir.dt.int32
+U32 = mybir.dt.uint32
+U16 = mybir.dt.uint16
+U8 = mybir.dt.uint8
+FP8X4 = mybir.dt.float8_e4m3fn_x4
+ACT = mybir.ActivationFunctionType
+ALU = mybir.AluOpType
+
+P = 128
+PACK = 4
+CHUNK = 256
+HALF = 512
+QUARTER = 256
+BIG = 3.0e38
+
+
+def tile_picked_laylerppagem_none_po_kernel(
+    tc, x_words, x_scales, w1_words, w1_scales, gn, w2_words, w2_scales, mem, offs, n1, n2, n3, n4, n5, out_0, out_1, out_2
+):
+    nc = tc.nc
+    with ExitStack() as ctx:
+        held = ctx.enter_context(tc.tile_pool(name="held", bufs=1))
+        psum = ctx.enter_context(tc.psum_pool(name="psum", bufs=1))
+
+        def sb(name, shape, dtype):
+            return held.tile(shape, dtype, name=name, align_bytes=64)
+
+        def load_list(name, src):
+            dst = held.tile([P, src.shape[1]], U16, name=name)
+            nc.sync.dma_start(dst[:], src)
+            return dst
+
+        def load_words(name, src):
+            dst = sb(name, [P, src.shape[2]], U32)
+            nc.sync.dma_start(dst[:].bitcast(I32), src[0].rearrange("p n t -> p (n t)").bitcast(I32))
+            return dst
+
+        def zeroed_plane(name, src, engine):
+            dst = sb(name, [P, src.shape[2]], U8)
+            engine.memset(dst[:].bitcast(I32), 0)
+            return dst
+
+        def load_scale_rows(dst, src, q, queue):
+            queue.dma_start(dst[32 * q : 32 * q + 4, :].bitcast(I32), src[0, 4 * q : 4 * q + 4, :].bitcast(I32))
+
+        def piece(lst, start, n):
+            return lst[:, start // 16 : (start + n) // 16]
+
+        xs = zeroed_plane("xs", x_scales, nc.vector)
+        w1s_raw = zeroed_plane("w1s_raw", w1_scales, nc.vector)
+        w2s_raw = zeroed_plane("w2s_raw", w2_scales, nc.vector)
+
+        l0 = load_list("l0", offs)
+        gain = sb("gain", [P, PACK], F32)
+        nc.sync.dma_start(gain[:], gn.rearrange("(p t) o -> p (t o)", t=PACK))
+        for q in range(4):
+            load_scale_rows(xs, x_scales, q, nc.sync if q < 2 else nc.scalar)
+        xw = load_words("xw", x_words)
+        w1_raw = load_words("w1_raw", w1_words)
+        for q in range(4):
+            load_scale_rows(w1s_raw, w1_scales, q, nc.sync if q < 2 else nc.scalar)
+        l2 = load_list("l2", n2)
+        l1 = load_list("l1", n1)
+        l3 = load_list("l3", n3)
+        for q in range(4):
+            load_scale_rows(w2s_raw, w2_scales, q, nc.sync)
+        w2_raw = load_words("w2_raw", w2_words)
+        l4 = load_list("l4", n4)
+        l5 = load_list("l5", n5)
+        mem_rows = mem.rearrange("(p t) w -> p t w", t=PACK)
+        page = [sb(f"page{t}", [P, U], F32) for t in range(PACK)]
+        for t in range(PACK):
+            nc.sync.dma_start(page[t][:], mem_rows[:, t, :])
+
+        def deal(name, raw_words, raw_scales, parts):
+            words = sb(name + "_words", [P, PACK, P], U32)
+            scales = sb(name + "_scales", [P, PACK, P], U8)
+            for lo, hi in parts:
+                nc.scalar.copy(words[:, lo:hi, :], raw_words[:].rearrange("p (m t) -> p t m", t=PACK)[:, lo:hi, :])
+                nc.vector.tensor_copy(scales[:, lo:hi, :], raw_scales[:].rearrange("p (m t) -> p t m", t=PACK)[:, lo:hi, :])
+            return words, scales
+
+        xsg = sb("xsg", [P, S], U8)
+        xg = sb("xg", [P, S], U32)
+        nc.vector.tensor_copy(xsg[:], xs[:].indirect(l0[:]))
+        nc.vector.tensor_copy(xg[:], xw[:].indirect(l0[:]))
+
+        w1, w1s = deal("w1", w1_raw, w1s_raw, [(0, 1), (1, PACK)])
+
+        safe = sb("safe", [P, PACK], F32)
+        inv = sb("inv", [P, PACK], F32)
+        ungain = sb("ungain", [P, PACK], F32)
+        nc.vector.scalar_tensor_tensor(safe[:], gain[:], 0.0, gain[:], ALU.is_equal, ALU.add)
+        nc.vector.reciprocal(inv[:], safe[:])
+        nc.vector.tensor_scalar(ungain[:], inv[:], BIG, -BIG, ALU.min, ALU.max)
+
+        scaled = [sb(f"scaled{t}", [P, S], F32) for t in range(PACK)]
+        for t in range(PACK):
+            y = psum.tile([P, S], F32, name=f"y{t}")
+            nc.tensor.matmul_mx(y[:], lhsT=w1[:, t, :].bitcast(FP8X4), lhsT_scale=w1s[:, t, :],
+                                rhs=xg[:].bitcast(FP8X4), rhs_scale=xsg[:], start=True, stop=True)
+            if t == PACK - 1:
+                nc.scalar.activation(scaled[t][:], y[:], ACT.Copy, scale=gain[:, t : t + 1])
+            else:
+                nc.vector.tensor_scalar(scaled[t][:], y[:], gain[:, t : t + 1], None, ALU.mult)
+
+        zq = sb("zq", [P, S], U32)
+        zs = sb("zs", [P, S], U8)
+
+        def mix(c):
+            c0 = c * CHUNK
+            a = sb(f"a{c}", [P, PACK, CHUNK], F32)
+            d = sb(f"d{c}", [P, PACK, CHUNK], F32)
+            m = sb(f"m{c}", [P, PACK, CHUNK], F32)
+            sg = sb(f"sg{c}", [P, PACK, CHUNK], F32)
+            for t in range(PACK):
+                picked = scaled[t][:].indirect(piece(l1, c0, CHUNK))
+                if c == 0 and t < 2:
+                    nc.vector.tensor_copy(a[:, t, :], picked)
+                else:
+                    nc.scalar.activation(a[:, t, :], picked, ACT.Copy)
+                nc.scalar.activation(sg[:, t, :], scaled[t][:].indirect(piece(l2, c0, CHUNK)), ACT.Sigmoid,
+                                     scale=ungain[:, t : t + 1])
+                nc.vector.tensor_tensor(d[:, t, :], scaled[t][:].indirect(piece(l3, c0, CHUNK)), a[:, t, :], ALU.subtract)
+                if t % 2 == 1:
+                    nc.vector.tensor_tensor(m[:, t - 1 : t + 1, :], d[:, t - 1 : t + 1, :], sg[:, t - 1 : t + 1, :], ALU.mult)
+            zb = sb(f"zb{c}", [P, CHUNK, PACK], BF16)
+            nc.vector.tensor_tensor(
+                zb[:].rearrange("p (c i) t -> p c t i", i=2),
+                a[:].rearrange("p t (c i) -> p c t i", i=2),
+                m[:].rearrange("p t (c i) -> p c t i", i=2),
+                ALU.add,
+            )
+            cols = slice(c0, c0 + CHUNK)
+            nc.vector.quantize_mx(zq[:, cols].bitcast(FP8X4), zs[:, cols], zb[:].rearrange("p n t -> p (n t)"))
+            return m
+
+        def project(acc, t, cols):
+            nc.tensor.matmul_mx(acc, lhsT=w2[:, t, :].bitcast(FP8X4), lhsT_scale=w2s[:, t, :],
+                                rhs=zq[:, cols].bitcast(FP8X4), rhs_scale=zs[:, cols], start=True, stop=True)
+
+        mix(0)
+        w2, w2s = deal("w2", w2_raw, w2s_raw, [(0, PACK)])
+        early = psum.tile([P, CHUNK], F32, name="y0")
+        project(early[:], 0, slice(0, CHUNK))
+        spent = mix(1)
+        late = psum.tile([P, CHUNK], F32, name="acc0")
+        project(late[:], 0, slice(CHUNK, S))
+        h = sb("h", [P, PACK, S], F32)
+        accs = []
+        for t in range(1, PACK):
+            acc = psum.tile([P, S], F32, name=f"acc{t}")
+            project(acc[:], t, slice(0, S))
+            accs.append(acc)
+        nc.scalar.copy(spent[:, 0, :], early[:])
+        nc.scalar.copy(h[:, 0, CHUNK:S], late[:])
+        for t in range(1, PACK):
+            nc.scalar.copy(h[:, t, :], accs[t - 1][:])
+
+        left = sb("left", [P, PACK, HALF], F32)
+        far_left = sb("far_left", [P, PACK - 1, HALF], F32)
+        ring = sb("ring", [P, PACK + 1, HALF], F32)
+        out_rows = out_0.rearrange("(p t) w -> p t w", t=PACK)
+
+        def far(t, u):
+            if u == 1:
+                return ring[:, t + 1, :]
+            return ring[:, 0, :] if t == PACK - 1 else far_left[:, t, :]
+
+        def blend(t, u):
+            cols = slice(u * HALF, (u + 1) * HALF)
+            res = ring[:, t, :] if u == 1 else left[:, t, :]
+            nc.vector.scalar_tensor_tensor(res, far(t, u), -0.5, page[t][:, cols], ALU.mult, ALU.add)
+            nc.sync.dma_start(out_rows[:, t, cols], res)
+
+        for t in range(PACK):
+            if t == 0:
+                nc.vector.tensor_copy(page[0][:].indirect(piece(l4, 0, CHUNK)), spent[:, 0, :])
+                nc.vector.tensor_copy(page[0][:].indirect(piece(l4, CHUNK, CHUNK)), h[:, 0, CHUNK:S])
+            else:
+                nc.vector.tensor_copy(page[t][:].indirect(l4[:]), h[:, t, :])
+            for u in range(2):
+                nc.scalar.activation(far(t, u), page[t][:].indirect(piece(l5, u * HALF, HALF)), ACT.Copy)
+
+        codes = sb("codes", [P, U], U32)
+        plane = sb("plane", [P, U], U8)
+        words_out = out_1[0].rearrange("p n t -> p (n t)").bitcast(I32)
+        for j in range(U // QUARTER):
+            if j % 2 == 0:
+                for t in range(PACK):
+                    blend(t, j // 2)
+            cols = slice(j * QUARTER, (j + 1) * QUARTER)
+            rb = sb(f"rb{j}", [P, QUARTER, PACK], BF16)
+            dst = rb[:].rearrange("p (c i) t -> p c t i", i=2)
+            rows = left if j < 2 else ring
+            src = rows[:, 0:PACK, (j % 2) * QUARTER : (j % 2 + 1) * QUARTER].rearrange("p t (c i) -> p c t i", i=2)
+            if j < 3:
+                nc.scalar.copy(dst, src)
+            else:
+                nc.vector.tensor_copy(dst, src)
+            nc.vector.quantize_mx(codes[:, cols].bitcast(FP8X4), plane[:, cols], rb[:].rearrange("p n t -> p (n t)"))
+            nc.sync.dma_start(words_out[:, cols], codes[:, cols].bitcast(I32))
+        for q in range(4):
+            queue = nc.sync if q % 2 == 0 else nc.scalar
+            queue.dma_start(out_2[0, 4 * q : 4 * q + 4, :].bitcast(I32), plane[32 * q : 32 * q + 4, :].bitcast(I32))

@@ -166,21 +166,23 @@ def tile_picked_laylerppagem_none_po_kernel(
         for t in range(1, PACK):
             nc.scalar.copy(h[:, t, :], accs[t - 1][:])
 
-        left = sb("left", [P, PACK, HALF], F32)
-        far_left = sb("far_left", [P, PACK - 1, HALF], F32)
-        ring = sb("ring", [P, PACK + 1, HALF], F32)
+        res = sb("res", [P, PACK, U], F32)
+        far = sb("far", [P, PACK, U], F32)
         out_rows = out_0.rearrange("(p t) w -> p t w", t=PACK)
 
-        def far(t, u):
-            if u == 1:
-                return ring[:, t + 1, :]
-            return ring[:, 0, :] if t == PACK - 1 else far_left[:, t, :]
+        def fetch(t, u):
+            cols = slice(u * HALF, (u + 1) * HALF)
+            picked = page[t][:].indirect(piece(l5, u * HALF, HALF))
+            if (t, u) == (PACK - 1, 1):
+                nc.vector.tensor_scalar(far[:, t, cols], picked, -0.5, 0.0, ALU.mult, ALU.add)
+            else:
+                nc.scalar.activation(far[:, t, cols], picked, ACT.Copy, scale=-0.5)
 
         def blend(t, u):
             cols = slice(u * HALF, (u + 1) * HALF)
-            res = ring[:, t, :] if u == 1 else left[:, t, :]
-            nc.vector.scalar_tensor_tensor(res, far(t, u), -0.5, page[t][:, cols], ALU.mult, ALU.add)
-            nc.sync.dma_start(out_rows[:, t, cols], res)
+            engine = nc.vector if t == PACK - 1 else nc.gpsimd
+            engine.tensor_tensor(res[:, t, cols], far[:, t, cols], page[t][:, cols], ALU.add)
+            nc.sync.dma_start(out_rows[:, t, cols], res[:, t, cols])
 
         for t in range(PACK):
             if t == 0:
@@ -189,26 +191,30 @@ def tile_picked_laylerppagem_none_po_kernel(
             else:
                 nc.vector.tensor_copy(page[t][:].indirect(l4[:]), h[:, t, :])
             for u in range(2):
-                nc.scalar.activation(far(t, u), page[t][:].indirect(piece(l5, u * HALF, HALF)), ACT.Copy)
+                fetch(t, u)
+            for u in range(2):
+                blend(t, 1 - u if t == PACK - 1 else u)
 
         codes = sb("codes", [P, U], U32)
         plane = sb("plane", [P, U], U8)
         words_out = out_1[0].rearrange("p n t -> p (n t)").bitcast(I32)
+        rounded = []
         for j in range(U // QUARTER):
-            if j % 2 == 0:
-                for t in range(PACK):
-                    blend(t, j // 2)
             cols = slice(j * QUARTER, (j + 1) * QUARTER)
             rb = sb(f"rb{j}", [P, QUARTER, PACK], BF16)
             dst = rb[:].rearrange("p (c i) t -> p c t i", i=2)
-            rows = left if j < 2 else ring
-            src = rows[:, 0:PACK, (j % 2) * QUARTER : (j % 2 + 1) * QUARTER].rearrange("p t (c i) -> p c t i", i=2)
-            if j < 3:
+            src = res[:, :, cols].rearrange("p t (c i) -> p c t i", i=2)
+            if j >= 2:
                 nc.scalar.copy(dst, src)
             else:
                 nc.vector.tensor_copy(dst, src)
-            nc.vector.quantize_mx(codes[:, cols].bitcast(FP8X4), plane[:, cols], rb[:].rearrange("p n t -> p (n t)"))
-            nc.sync.dma_start(words_out[:, cols], codes[:, cols].bitcast(I32))
+            rounded.append(rb)
+        for j in range(U // QUARTER):
+            cols = slice(j * QUARTER, (j + 1) * QUARTER)
+            nc.vector.quantize_mx(codes[:, cols].bitcast(FP8X4), plane[:, cols], rounded[j][:].rearrange("p n t -> p (n t)"))
+            if j > 0:
+                done = slice(0 if j == 1 else j * QUARTER, (j + 1) * QUARTER)
+                nc.sync.dma_start(words_out[:, done], codes[:, done].bitcast(I32))
         for q in range(4):
             queue = nc.sync if q % 2 == 0 else nc.scalar
             queue.dma_start(out_2[0, 4 * q : 4 * q + 4, :].bitcast(I32), plane[32 * q : 32 * q + 4, :].bitcast(I32))

from contextlib import ExitStack

import concourse.mybir as mybir

K, T, S, N, H, U = 512, 2048, 512, 512, 512, 1024
FLOPS = 2 * K * H * S + 2 * H * N * S

F32 = mybir.dt.float32
BF16 = mybir.dt.bfloat16
I32 = mybir.dt.int32
U32 = mybir.dt.uint32
U16 = mybir.dt.uint16
U8 = mybir.dt.uint8
FP8X4 = mybir.dt.float8_e4m3fn_x4
ACT = mybir.ActivationFunctionType
ALU = mybir.AluOpType

P = 128
PACK = 4
CHUNK = 256
HALF = 512
QUARTER = 256
BIG = 3.0e38


def tile_picked_laylerppagem_none_po_kernel(
    tc, x_words, x_scales, w1_words, w1_scales, gn, w2_words, w2_scales, mem, offs, n1, n2, n3, n4, n5, out_0, out_1, out_2
):
    nc = tc.nc
    with ExitStack() as ctx:
        held = ctx.enter_context(tc.tile_pool(name="held", bufs=1))
        psum = ctx.enter_context(tc.psum_pool(name="psum", bufs=1))

        def sb(name, shape, dtype):
            return held.tile(shape, dtype, name=name, align_bytes=64)

        def load_list(name, src):
            dst = held.tile([P, src.shape[1]], U16, name=name)
            nc.sync.dma_start(dst[:], src)
            return dst

        def load_words(name, src):
            dst = sb(name, [P, src.shape[2]], U32)
            nc.sync.dma_start(dst[:].bitcast(I32), src[0].rearrange("p n t -> p (n t)").bitcast(I32))
            return dst

        def zeroed_plane(name, src, engine):
            dst = sb(name, [P, src.shape[2]], U8)
            engine.memset(dst[:].bitcast(I32), 0)
            return dst

        def load_scale_rows(dst, src, q, queue):
            queue.dma_start(dst[32 * q : 32 * q + 4, :].bitcast(I32), src[0, 4 * q : 4 * q + 4, :].bitcast(I32))

        def piece(lst, start, n):
            return lst[:, start // 16 : (start + n) // 16]

        xs = zeroed_plane("xs", x_scales, nc.vector)
        w1s_raw = zeroed_plane("w1s_raw", w1_scales, nc.vector)
        w2s_raw = zeroed_plane("w2s_raw", w2_scales, nc.vector)

        l0 = load_list("l0", offs)
        gain = sb("gain", [P, PACK], F32)
        nc.sync.dma_start(gain[:], gn.rearrange("(p t) o -> p (t o)", t=PACK))
        for q in range(4):
            load_scale_rows(xs, x_scales, q, nc.sync if q < 2 else nc.scalar)
        xw = load_words("xw", x_words)
        w1_raw = load_words("w1_raw", w1_words)
        for q in range(4):
            load_scale_rows(w1s_raw, w1_scales, q, nc.sync if q < 2 else nc.scalar)
        l2 = load_list("l2", n2)
        l1 = load_list("l1", n1)
        l3 = load_list("l3", n3)
        for q in range(4):
            load_scale_rows(w2s_raw, w2_scales, q, nc.sync)
        w2_raw = load_words("w2_raw", w2_words)
        l4 = load_list("l4", n4)
        l5 = load_list("l5", n5)
        mem_rows = mem.rearrange("(p t) w -> p t w", t=PACK)
        page = [sb(f"page{t}", [P, U], F32) for t in range(PACK)]
        for t in range(PACK):
            nc.sync.dma_start(page[t][:], mem_rows[:, t, :])

        def deal(name, raw_words, raw_scales, parts):
            words = sb(name + "_words", [P, PACK, P], U32)
            scales = sb(name + "_scales", [P, PACK, P], U8)
            for lo, hi in parts:
                nc.scalar.copy(words[:, lo:hi, :], raw_words[:].rearrange("p (m t) -> p t m", t=PACK)[:, lo:hi, :])
                nc.vector.tensor_copy(scales[:, lo:hi, :], raw_scales[:].rearrange("p (m t) -> p t m", t=PACK)[:, lo:hi, :])
            return words, scales

        xsg = sb("xsg", [P, S], U8)
        xg = sb("xg", [P, S], U32)
        nc.vector.tensor_copy(xsg[:], xs[:].indirect(l0[:]))
        nc.vector.tensor_copy(xg[:], xw[:].indirect(l0[:]))

        w1, w1s = deal("w1", w1_raw, w1s_raw, [(0, 1), (1, PACK)])

        safe = sb("safe", [P, PACK], F32)
        inv = sb("inv", [P, PACK], F32)
        ungain = sb("ungain", [P, PACK], F32)
        nc.vector.scalar_tensor_tensor(safe[:], gain[:], 0.0, gain[:], ALU.is_equal, ALU.add)
        nc.vector.reciprocal(inv[:], safe[:])
        nc.vector.tensor_scalar(ungain[:], inv[:], BIG, -BIG, ALU.min, ALU.max)

        scaled = [sb(f"scaled{t}", [P, S], F32) for t in range(PACK)]
        for t in range(PACK):
            y = psum.tile([P, S], F32, name=f"y{t}")
            nc.tensor.matmul_mx(y[:], lhsT=w1[:, t, :].bitcast(FP8X4), lhsT_scale=w1s[:, t, :],
                                rhs=xg[:].bitcast(FP8X4), rhs_scale=xsg[:], start=True, stop=True)
            if t == PACK - 1:
                nc.scalar.activation(scaled[t][:], y[:], ACT.Copy, scale=gain[:, t : t + 1])
            else:
                nc.vector.tensor_scalar(scaled[t][:], y[:], gain[:, t : t + 1], None, ALU.mult)

        zq = sb("zq", [P, S], U32)
        zs = sb("zs", [P, S], U8)

        def mix(c):
            c0 = c * CHUNK
            a = sb(f"a{c}", [P, PACK, CHUNK], F32)
            d = sb(f"d{c}", [P, PACK, CHUNK], F32)
            m = sb(f"m{c}", [P, PACK, CHUNK], F32)
            sg = sb(f"sg{c}", [P, PACK, CHUNK], F32)
            for t in range(PACK):
                picked = scaled[t][:].indirect(piece(l1, c0, CHUNK))
                if c == 0 and t < 2:
                    nc.vector.tensor_copy(a[:, t, :], picked)
                else:
                    nc.scalar.activation(a[:, t, :], picked, ACT.Copy)
                nc.scalar.activation(sg[:, t, :], scaled[t][:].indirect(piece(l2, c0, CHUNK)), ACT.Sigmoid,
                                     scale=ungain[:, t : t + 1])
                nc.vector.tensor_tensor(d[:, t, :], scaled[t][:].indirect(piece(l3, c0, CHUNK)), a[:, t, :], ALU.subtract)
                if t % 2 == 1:
                    nc.vector.tensor_tensor(m[:, t - 1 : t + 1, :], d[:, t - 1 : t + 1, :], sg[:, t - 1 : t + 1, :], ALU.mult)
            zb = sb(f"zb{c}", [P, CHUNK, PACK], BF16)
            nc.vector.tensor_tensor(
                zb[:].rearrange("p (c i) t -> p c t i", i=2),
                a[:].rearrange("p t (c i) -> p c t i", i=2),
                m[:].rearrange("p t (c i) -> p c t i", i=2),
                ALU.add,
            )
            cols = slice(c0, c0 + CHUNK)
            nc.vector.quantize_mx(zq[:, cols].bitcast(FP8X4), zs[:, cols], zb[:].rearrange("p n t -> p (n t)"))
            return m

        def project(acc, t, cols):
            nc.tensor.matmul_mx(acc, lhsT=w2[:, t, :].bitcast(FP8X4), lhsT_scale=w2s[:, t, :],
                                rhs=zq[:, cols].bitcast(FP8X4), rhs_scale=zs[:, cols], start=True, stop=True)

        mix(0)
        w2, w2s = deal("w2", w2_raw, w2s_raw, [(0, PACK)])
        early = psum.tile([P, CHUNK], F32, name="y0")
        project(early[:], 0, slice(0, CHUNK))
        spent = mix(1)
        late = psum.tile([P, CHUNK], F32, name="acc0")
        project(late[:], 0, slice(CHUNK, S))
        h = sb("h", [P, PACK, S], F32)
        accs = []
        for t in range(1, PACK):
            acc = psum.tile([P, S], F32, name=f"acc{t}")
            project(acc[:], t, slice(0, S))
            accs.append(acc)
        nc.scalar.copy(spent[:, 0, :], early[:])
        nc.scalar.copy(h[:, 0, CHUNK:S], late[:])
        for t in range(1, PACK):
            nc.scalar.copy(h[:, t, :], accs[t - 1][:])

        res = sb("res", [P, PACK, U], F32)
        far = sb("far", [P, PACK, U], F32)
        out_rows = out_0.rearrange("(p t) w -> p t w", t=PACK)

        def fetch(t, u):
            cols = slice(u * HALF, (u + 1) * HALF)
            picked = page[t][:].indirect(piece(l5, u * HALF, HALF))
            if (t, u) == (PACK - 1, 1):
                nc.vector.tensor_scalar(far[:, t, cols], picked, -0.5, 0.0, ALU.mult, ALU.add)
            else:
                nc.scalar.activation(far[:, t, cols], picked, ACT.Copy, scale=-0.5)

        def blend(t, u):
            cols = slice(u * HALF, (u + 1) * HALF)
            engine = nc.vector if t == PACK - 1 else nc.gpsimd
            engine.tensor_tensor(res[:, t, cols], far[:, t, cols], page[t][:, cols], ALU.add)
            nc.sync.dma_start(out_rows[:, t, cols], res[:, t, cols])

        for t in range(PACK):
            if t == 0:
                nc.vector.tensor_copy(page[0][:].indirect(piece(l4, 0, CHUNK)), spent[:, 0, :])
                nc.vector.tensor_copy(page[0][:].indirect(piece(l4, CHUNK, CHUNK)), h[:, 0, CHUNK:S])
            else:
                nc.vector.tensor_copy(page[t][:].indirect(l4[:]), h[:, t, :])
            for u in range(2):
                fetch(t, u)
            for u in range(2):
                blend(t, 1 - u if t == PACK - 1 else u)

        codes = sb("codes", [P, U], U32)
        plane = sb("plane", [P, U], U8)
        words_out = out_1[0].rearrange("p n t -> p (n t)").bitcast(I32)
        rounded = []
        for j in range(U // QUARTER):
            cols = slice(j * QUARTER, (j + 1) * QUARTER)
            rb = sb(f"rb{j}", [P, QUARTER, PACK], BF16)
            dst = rb[:].rearrange("p (c i) t -> p c t i", i=2)
            src = res[:, :, cols].rearrange("p t (c i) -> p c t i", i=2)
            if j >= 2:
                nc.scalar.copy(dst, src)
            else:
                nc.vector.tensor_copy(dst, src)
            rounded.append(rb)
        for j in range(U // QUARTER):
            cols = slice(j * QUARTER, (j + 1) * QUARTER)
            nc.vector.quantize_mx(codes[:, cols].bitcast(FP8X4), plane[:, cols], rounded[j][:].rearrange("p n t -> p (n t)"))
            if j > 0:
                done = slice(0 if j == 1 else j * QUARTER, (j + 1) * QUARTER)
                nc.sync.dma_start(words_out[:, done], codes[:, done].bitcast(I32))
        for q in range(4):
            queue = nc.sync if q % 2 == 0 else nc.scalar
            queue.dma_start(out_2[0, 4 * q : 4 * q + 4, :].bitcast(I32), plane[32 * q : 32 * q + 4, :].bitcast(I32))
